import numpy as np
import ml_dtypes


def mxq(x, axis, fmt="e4m3"):
    dtype, down = {"e4m3": (ml_dtypes.float8_e4m3fn, 7), "e5m2": (ml_dtypes.float8_e5m2, 14)}[fmt]
    v = np.moveaxis(np.asarray(x, np.float32).astype(ml_dtypes.bfloat16).astype(np.float64), axis, -1)
    blocks = v.reshape(v.shape[:-1] + (-1, 32))
    amax = np.abs(blocks).max(-1, keepdims=True)
    byte = np.maximum(np.where(amax > 0, np.frexp(amax)[1] - 1 + 127, 0) - down, 1)
    scale = np.exp2(byte - 127.0)
    codes = (blocks / scale).astype(np.float32).astype(dtype).astype(np.float64)
    return np.moveaxis((codes * scale).reshape(v.shape), -1, axis)


WIDE = False


def mx_kscale(k):
    if not WIDE:
        return np.ones(k)
    levels = np.array([10, -10, 5, -5, 0])
    if k % 512:
        return np.exp2(np.random.permutation(np.resize(levels, k // 32))).repeat(32)
    a = np.empty((k // 512, 16))
    for p in range(k // 512):
        a[p, :8] = np.random.permutation(np.resize(levels, 8))
        for g in range(8):
            far = levels[np.abs(levels - a[p, g]) >= 10]
            a[p, g + 8] = far[np.random.randint(len(far))]
    return np.exp2(a.ravel()).repeat(32)


def f64(x):
    return np.asarray(x).astype(np.float64)


def striped(idx):
    return np.tile(np.asarray(idx).reshape(-1, 16).T, (8, 1)).astype(np.uint16)


def unstriped(offs):
    return offs[:16].T.reshape(-1).astype(np.int64)


E2M1 = np.array([0.0, 0.5, 1.0, 1.5, 2.0, 3.0, 4.0, 6.0, -0.0, -0.5, -1.0, -1.5, -2.0, -3.0, -4.0, -6.0])


def pack_weight(w, fmt):
    k, n = w.shape
    w = f64(np.asarray(w, np.float32).astype(ml_dtypes.bfloat16)).reshape(k // 32, 32, n)
    amax = np.abs(w).max(1)
    if fmt == "e4m3":
        byte = np.frexp(amax)[1] - 1 + 127 - 7
    else:
        mant, ex = np.frexp(amax / 6.0)
        byte = np.where(mant > 0.5, ex, ex - 1) + 127
    byte = np.clip(np.where(amax > 0, byte, 1), 1, 254)
    scaled = (w * np.exp2(127.0 - byte)[:, None, :]).reshape(k, n).astype(np.float32)
    by_word = np.ascontiguousarray(scaled.reshape(k // 512, 128, 4, n).transpose(0, 1, 3, 2))
    if fmt == "e4m3":
        words = by_word.astype(ml_dtypes.float8_e4m3fn).view(np.uint8)
    else:
        c = by_word.astype(ml_dtypes.float4_e2m1fn).view(np.uint8) & 0xF
        words = (c[..., 0::2] | (c[..., 1::2] << 4)).reshape(k // 512, 128, 2 * n)
    return np.ascontiguousarray(words), np.ascontiguousarray(byte.astype(np.uint8).reshape(k // 512, 16, n))


def unpack_weight(words, scales, fmt):
    g, _, n = scales.shape
    words = np.ascontiguousarray(words).reshape(g, 128, n, -1)
    if fmt == "e4m3":
        vals = words.view(ml_dtypes.float8_e4m3fn).astype(np.float64)
    else:
        nib = np.empty((g, 128, n, 4), np.uint8)
        nib[..., 0::2] = words & 0xF
        nib[..., 1::2] = words >> 4
        vals = E2M1[nib]
    vals = vals * np.repeat(np.exp2(scales.astype(np.float64) - 127.0), 8, axis=1)[..., None]
    return vals.transpose(0, 1, 3, 2).reshape(g * 512, n)


D, T, I, Q, E, U, M = 512, 2048, 512, 256, 512, 1024, 1024


def setup_inputs():
    n = np.random.standard_normal
    idx = np.random.permutation(T)[:I]
    idx2 = np.random.permutation(U)[:I]
    idx3 = np.random.permutation(M)[:Q]
    fd = mx_kscale(D)
    fi = mx_kscale(I)
    ti = np.ones(T)
    ti[idx] = fi
    keysp = pack_weight(n((D, T)) / fd[:, None], "e4m3")
    return {
        "query": (n((D, Q)) * 0.9 / np.sqrt(D) * fd[:, None]).astype(np.float32),
        "keys_words": keysp[0],
        "keys_scales": keysp[1],
        "query2": (n((D, Q)) * 0.9 / np.sqrt(D) * fd[:, None]).astype(np.float32),
        "notes": (n((D, U)) / fd[:, None]).astype(np.float32),
        "lam": (np.random.uniform(0.1, 0.5, (Q, 1))).astype(np.float32),
        "os": (np.random.uniform(0.02, 0.08, (1, I)) * fi).astype(np.float32),
        "vals": (n((E, T)) / ti).astype(np.float32),
        "old": (n((E, M)) * 2.0).astype(np.float32),
        "fade": (np.random.uniform(0.3, 0.9, (1, M))).astype(np.float32),
        "offs": striped(idx),
        "offs2": striped(idx2),
        "offs3": striped(idx3),
    }


def reference(query, keys_words, keys_scales, query2, notes, lam, os, vals, old, fade, offs, offs2, offs3):
    idx = unstriped(offs)
    idx2 = unstriped(offs2)
    idx3 = unstriped(offs3)
    keysu = unpack_weight(keys_words, keys_scales, "e4m3")
    queryq = mxq(f64(query), 0, "e4m3")
    keysidxg = keysu[:, idx]
    a = queryq.T @ keysidxg
    query2q = mxq(f64(query2), 0, "e4m3")
    notesidx2q = mxq(f64(notes)[:, idx2], 0, "e4m3")
    b = query2q.T @ notesidx2q
    s = np.maximum(a, b) + np.minimum(a, b) * f64(lam)
    w = np.maximum(s, 0.0)
    wo1 = w * f64(os)
    wt1 = wo1.T
    vt1 = f64(vals)[:, idx].T
    vt1q = mxq(vt1, 0, "e4m3")
    wt1q = mxq(wt1, 0, "e4m3")
    o = vt1q.T @ wt1q
    of = np.zeros((E, M))
    of[:, idx3] = o
    y = f64(old) * f64(fade) + of
    return y

@@ -1,0 +1,270 @@
+from contextlib import ExitStack
+
+import concourse.mybir as mybir
+from concourse.masks import make_identity
+
+D, T, I, Q, E, U, M = 512, 2048, 512, 256, 512, 1024, 1024
+FLOPS = 2 * D * Q * I * 2 + 2 * I * E * Q
+
+F32 = mybir.dt.float32
+BF16 = mybir.dt.bfloat16
+I32 = mybir.dt.int32
+U32 = mybir.dt.uint32
+U16 = mybir.dt.uint16
+U8 = mybir.dt.uint8
+FP8X4 = mybir.dt.float8_e4m3fn_x4
+ALU = mybir.AluOpType
+COPY = mybir.ActivationFunctionType.Copy
+
+P = 128
+PACK = 4
+BANK = 512
+Q_TILES = Q // P
+E_TILES = E // P
+M_HALVES = M // BANK
+WORDS = I // 2
+HALF = I // 2
+LOAD_ORDER = (("v", 0), ("v", 1), ("v", 2), ("o", 0), ("o", 1), ("v", 3), ("o", 2), ("o", 3))
+
+
+def interleave(engine_copy, dst, src):
+    engine_copy(
+        dst.rearrange("p (c i) t -> p c t i", i=4),
+        src.rearrange("p t (c i) -> p c t i", i=4),
+    )
+
+
+def quantize(nc, codes, scales, grouped):
+    nc.vector.quantize_mx(out=codes.bitcast(FP8X4), scales=scales, in_=grouped)
+
+
+def product(nc, out, lhs_codes, lhs_scales, rhs_codes, rhs_scales):
+    nc.tensor.matmul_mx(
+        out=out,
+        lhsT=lhs_codes.bitcast(FP8X4),
+        lhsT_scale=lhs_scales,
+        rhs=rhs_codes.bitcast(FP8X4),
+        rhs_scale=rhs_scales,
+        start=True,
+        stop=True,
+    )
+
+
+def tile_attend_twopools_written_lean_kernel(
+    tc, query, keys_words, keys_scales, query2, notes, lam, slot_factor, vals, old, fade, offs, offs2, offs3, out
+):
+    nc = tc.nc
+    with ExitStack() as ctx:
+        sb = ctx.enter_context(tc.tile_pool(name="sb", bufs=1))
+        ps = ctx.enter_context(tc.psum_pool(name="ps", bufs=1))
+
+        def tile(name, shape, dtype):
+            return sb.tile(shape, dtype, name=name, align_bytes=64)
+
+        def bank(name):
+            return ps.tile([P, BANK], F32, name=name)
+
+        key_scale_pool = tile("key_scale_pool", [P, T], U8)
+        nc.vector.memset(key_scale_pool[:].bitcast(I32), 0)
+
+        note_list = tile("note_list", [P, I // 16], U16)
+        nc.sync.dma_start(note_list[:], offs2)
+        token_list = tile("token_list", [P, I // 16], U16)
+        nc.sync.dma_start(token_list[:], offs)
+        note_rows = notes.rearrange("(p t) u -> p t u", t=PACK)
+        note_pool = [tile("note_pool%d" % t, [P, U], F32) for t in range(PACK)]
+        for t in range(PACK):
+            nc.sync.dma_start(out=note_pool[t][:], in_=note_rows[:, t, :])
+        for g in range(4):
+            nc.scalar.dma_start(
+                out=key_scale_pool[32 * g : 32 * g + 4, :].bitcast(I32),
+                in_=keys_scales[0, 4 * g : 4 * g + 4, :].bitcast(I32),
+            )
+        q2_raw = tile("q2_raw", [P, PACK, Q], F32)
+        nc.sync.dma_start(out=q2_raw[:], in_=query2.rearrange("(p t) q -> p t q", t=PACK))
+        q1_raw = tile("q1_raw", [P, PACK, Q], F32)
+        nc.sync.dma_start(out=q1_raw[:], in_=query.rearrange("(p t) q -> p t q", t=PACK))
+        key_word_pool = tile("key_word_pool", [P, T], U32)
+        nc.sync.dma_start(
+            out=key_word_pool[:].bitcast(I32), in_=keys_words[0].rearrange("p n t -> p (n t)").bitcast(I32)
+        )
+        place_list = tile("place_list", [P, Q // 16], U16)
+        nc.sync.dma_start(place_list[:], offs3)
+
+        factor_cols = tile("factor_cols", [P, PACK], F32)
+        nc.gpsimd.dma_start(out=factor_cols[:], in_=slot_factor.rearrange("o (p j) -> p (o j)", j=PACK))
+        lam_cols = tile("lam_cols", [P, Q_TILES], F32)
+        with nc.allow_non_contiguous_dma(reason="one float32 a partition and query tile"):
+            nc.gpsimd.dma_start(out=lam_cols[:], in_=lam.rearrange("(h p) o -> p (h o)", p=P))
+        fade_cols = tile("fade_cols", [P, M_HALVES, PACK], F32)
+        nc.gpsimd.dma_start(out=fade_cols[:], in_=fade.rearrange("o (h p j) -> p (o h) j", h=M_HALVES, j=PACK))
+
+        val_pool = [tile("val_pool%d" % j, [P, T], F32) for j in range(E_TILES)]
+        old_rows = [tile("old_rows%d" % j, [P, M], F32) for j in range(E_TILES)]
+        for kind, j in LOAD_ORDER:
+            if kind == "v":
+                nc.sync.dma_start(out=val_pool[j][:], in_=vals[P * j : P * (j + 1), :])
+            else:
+                nc.sync.dma_start(out=old_rows[j][:], in_=old[P * j : P * (j + 1), :])
+
+        placed = [tile("placed%d" % n, [P, M], F32) for n in range(2)]
+        for n in range(2):
+            nc.vector.memset(placed[n][:], 0.0)
+        ident = tile("ident", [P, P], F32)
+        make_identity(nc, ident[:])
+
+        key_codes = tile("key_codes", [P, I], U32)
+        key_scales = tile("key_scales", [P, I], U8)
+        nc.vector.tensor_copy(key_scales[:], key_scale_pool[:].indirect(token_list[:]))
+
+        note_planes = tile("note_planes", [P, PACK, I], BF16)
+        for t in range(PACK):
+            picked = note_pool[t][:].indirect(note_list[:])
+            if t < 2:
+                nc.scalar.activation(note_planes[:, t, :], picked, COPY)
+            else:
+                nc.vector.tensor_copy(note_planes[:, t, :], picked)
+        note_grouped = tile("note_grouped", [P, I, PACK], BF16)
+        interleave(nc.vector.tensor_copy, note_grouped[:], note_planes[:])
+        note_codes = tile("note_codes", [P, I], U32)
+        note_scales = tile("note_scales", [P, I], U8)
+        quantize(nc, note_codes[:], note_scales[:], note_grouped[:].rearrange("p s t -> p (s t)"))
+
+        q_codes, q_scales = [], []
+        for n, raw in enumerate((q2_raw, q1_raw)):
+            grouped = tile("q_grouped%d" % n, [P, Q, PACK], BF16)
+            interleave(nc.scalar.copy, grouped[:], raw[:])
+            q_codes.append(tile("q_codes%d" % n, [P, Q], U32))
+            q_scales.append(tile("q_scales%d" % n, [P, Q], U8))
+            quantize(nc, q_codes[n][:], q_scales[n][:], grouped[:].rearrange("p q t -> p (q t)"))
+
+
+        fade_bank = [bank("fade_bank%d" % h) for h in range(M_HALVES)]
+        for h in range(M_HALVES):
+            for j in range(PACK):
+                nc.tensor.transpose(
+                    fade_bank[h][:, P * j : P * (j + 1)], fade_cols[:, h, j : j + 1].to_broadcast([P, P]), ident[:]
+                )
+
+        a_bank = [bank("a_bank%d" % n) for n in range(2)]
+        b_bank = [bank("b_bank%d" % n) for n in range(2)]
+        b_dealt = tile("b_dealt", [P, Q_TILES * I], F32)
+        smaller = tile("smaller", [P, Q_TILES * I], F32)
+        larger = tile("larger", [P, Q_TILES * I], F32)
+        faded = [tile("faded%d" % n, [P, M], F32) for n in range(2)]
+
+        def scores(banks, n, which, codes, scales):
+            slots = slice(HALF * n, HALF * (n + 1))
+            for h in range(Q_TILES):
+                rows = slice(P * h, P * (h + 1))
+                product(
+                    nc,
+                    banks[n][:, HALF * h : HALF * (h + 1)],
+                    q_codes[which][:, rows],
+                    q_scales[which][:, rows],
+                    codes[:, slots],
+                    scales[:, slots],
+                )
+
+        def dealt_from_bank(bank_tile):
+            return bank_tile[:].rearrange("q (h p t) -> q h t p", h=Q_TILES, t=PACK)
+
+        def dealt_half(rows, n):
+            return rows[:].rearrange("q (h t p) -> q h t p", h=Q_TILES, t=PACK)[:, :, :, P // 2 * n : P // 2 * (n + 1)]
+
+        for n in range(2):
+            scores(b_bank, n, 0, note_codes, note_scales)
+            nc.scalar.copy(dealt_half(b_dealt, n), dealt_from_bank(b_bank[n]))
+        for n in range(2):
+            entries = token_list[:, HALF // 16 * n : HALF // 16 * (n + 1)]
+            nc.vector.tensor_copy(key_codes[:, HALF * n : HALF * (n + 1)], key_word_pool[:].indirect(entries))
+            scores(a_bank, n, 1, key_codes, key_scales)
+        for n in range(2):
+            for dst, op in ((smaller, ALU.min), (larger, ALU.max)):
+                nc.vector.tensor_tensor(dealt_half(dst, n), dealt_from_bank(a_bank[n]), dealt_half(b_dealt, n), op)
+        for h in range(Q_TILES):
+            cols = slice(I * h, I * (h + 1))
+            nc.vector.scalar_tensor_tensor(
+                larger[:, cols], smaller[:, cols], lam_cols[:, h : h + 1], larger[:, cols], ALU.mult, ALU.add
+            )
+            for t in range(PACK):
+                nc.tensor.transpose(
+                    b_bank[h][:, P * t : P * (t + 1)], larger[:, I * h + P * t : I * h + P * (t + 1)], ident[:]
+                )
+        v_codes = tile("v_codes", [P, E], U32)
+        v_scales = tile("v_scales", [P, E], U8)
+        staged = [tile("staged%d" % n, [P, WORDS], F32) for n in range(2)]
+        first_staged = tile("first_staged", [P, WORDS], F32)
+
+        def gather_and_turn(j, words, turned):
+            nc.scalar.activation(words.bitcast(BF16), val_pool[j][:].indirect(token_list[:]), COPY)
+            for u in range(2):
+                nc.tensor.transpose(turned[:, P * u : P * (u + 1)], words[:, u:WORDS:2], ident[:])
+
+        def group_and_quantize(first, count, turned, grouped):
+            nc.vector.tensor_copy(
+                grouped.rearrange("p (j e u) -> p j e u", j=count, u=2),
+                turned.rearrange("p (j u e) -> p j e u", j=count, u=2),
+            )
+            cols = slice(P * first, P * (first + count))
+            quantize(nc, v_codes[:, cols], v_scales[:, cols], grouped.bitcast(BF16))
+
+        def read_and_place(j, o_bank):
+            cols = slice(P * j, P * (j + 1))
+            product(nc, o_bank[:, :Q], v_codes[:, cols], v_scales[:, cols], w_codes[:], w_scales[:])
+            nc.scalar.copy(staged[j % 2][:], o_bank[:, :Q])
+            nc.scalar.activation(placed[j % 2][:].indirect(place_list[:]), staged[j % 2][:], COPY)
+
+        def fade_old(j):
+            for h in range(M_HALVES):
+                cols = slice(BANK * h, BANK * (h + 1))
+                nc.vector.tensor_tensor(
+                    faded[j % 2][:, cols].rearrange("e (p i) -> e p i", i=PACK),
+                    old_rows[j][:, cols].rearrange("e (p i) -> e p i", i=PACK),
+                    fade_bank[h][:].rearrange("e (i p) -> e p i", i=PACK),
+                    ALU.mult,
+                )
+
+        def add_and_store(j, pieces):
+            result = old_rows[(j + 1) % E_TILES]
+            for n in range(pieces):
+                cols = slice(M // pieces * n, M // pieces * (n + 1))
+                nc.vector.tensor_tensor(result[:, cols], faded[j % 2][:, cols], placed[j % 2][:, cols], ALU.add)
+                nc.sync.dma_start(out=out[P * j : P * (j + 1), cols], in_=result[:, cols])
+
+        def middle(rows, words):
+            return rows[:, M // 2 - words // 2 : M // 2 + words // 2]
+
+        gather_and_turn(0, first_staged[:], a_bank[0][:, :WORDS])
+        group_and_quantize(0, 1, a_bank[0][:, :WORDS], middle(b_dealt, WORDS))
+        w_grouped = middle(faded[0], 2 * WORDS).bitcast(BF16)
+        for h in range(Q_TILES):
+            nc.vector.scalar_tensor_tensor(
+                w_grouped[:, I * h : I * (h + 1)].rearrange("p (q t) -> p q t", t=PACK),
+                b_bank[h][:].rearrange("p (t q) -> p q t", t=PACK),
+                0.0,
+                factor_cols[:].unsqueeze(1).to_broadcast([P, P, PACK]),
+                ALU.max,
+                ALU.mult,
+            )
+        w_codes = tile("w_codes", [P, Q], U32)
+        w_scales = tile("w_scales", [P, Q], U8)
+        quantize(nc, w_codes[:], w_scales[:], w_grouped)
+
+        gather_and_turn(1, staged[1][:], b_bank[1][:, :WORDS])
+        gather_and_turn(2, staged[0][:], b_bank[1][:, WORDS:])
+        read_and_place(0, a_bank[1])
+        fade_old(0)
+        group_and_quantize(1, 2, b_bank[1][:], middle(faded[1], 2 * WORDS))
+        fade_old(1)
+        add_and_store(0, 1)
+        gather_and_turn(3, staged[0][:], b_bank[0][:, :WORDS])
+        read_and_place(1, a_bank[0])
+        fade_old(2)
+        group_and_quantize(3, 1, b_bank[0][:, :WORDS], middle(old_rows[2], WORDS))
+        add_and_store(1, 1)
+        read_and_place(2, a_bank[1])
+        read_and_place(3, a_bank[0])
+        fade_old(3)
+        add_and_store(2, 1)
+        add_and_store(3, 2)

@@ -107,9 +107,9 @@ def tile_attend_twopools_written_lean_kernel(
             else:
                 nc.sync.dma_start(out=old_rows[j][:], in_=old[P * j : P * (j + 1), :])
 
-        placed = [tile("placed%d" % n, [P, M], F32) for n in range(2)]
-        for n in range(2):
-            nc.vector.memset(placed[n][:], 0.0)
+        placed = [tile("placed%d" % j, [P, M], F32) for j in range(E_TILES)]
+        for j in range(E_TILES):
+            nc.vector.memset(placed[j][:], 0.0)
         ident = tile("ident", [P, P], F32)
         make_identity(nc, ident[:])
 
@@ -197,7 +197,11 @@ def tile_attend_twopools_written_lean_kernel(
         first_staged = tile("first_staged", [P, WORDS], F32)
 
         def gather_and_turn(j, words, turned):
-            nc.scalar.activation(words.bitcast(BF16), val_pool[j][:].indirect(token_list[:]), COPY)
+            picked = val_pool[j][:].indirect(token_list[:])
+            if j < E_TILES - 1:
+                nc.scalar.activation(words.bitcast(BF16), picked, COPY)
+            else:
+                nc.vector.tensor_copy(words.bitcast(BF16), picked)
             for u in range(2):
                 nc.tensor.transpose(turned[:, P * u : P * (u + 1)], words[:, u:WORDS:2], ident[:])
 
@@ -213,24 +217,23 @@ def tile_attend_twopools_written_lean_kernel(
             cols = slice(P * j, P * (j + 1))
             product(nc, o_bank[:, :Q], v_codes[:, cols], v_scales[:, cols], w_codes[:], w_scales[:])
             nc.scalar.copy(staged[j % 2][:], o_bank[:, :Q])
-            nc.scalar.activation(placed[j % 2][:].indirect(place_list[:]), staged[j % 2][:], COPY)
+            nc.scalar.activation(placed[j][:].indirect(place_list[:]), staged[j % 2][:], COPY)
 
-        def fade_old(j):
+        def fade_old(j, faded_rows):
             for h in range(M_HALVES):
                 cols = slice(BANK * h, BANK * (h + 1))
                 nc.vector.tensor_tensor(
-                    faded[j % 2][:, cols].rearrange("e (p i) -> e p i", i=PACK),
+                    faded_rows[:, cols].rearrange("e (p i) -> e p i", i=PACK),
                     old_rows[j][:, cols].rearrange("e (p i) -> e p i", i=PACK),
                     fade_bank[h][:].rearrange("e (i p) -> e p i", i=PACK),
                     ALU.mult,
                 )
 
-        def add_and_store(j, pieces):
-            result = old_rows[(j + 1) % E_TILES]
-            for n in range(pieces):
-                cols = slice(M // pieces * n, M // pieces * (n + 1))
-                nc.vector.tensor_tensor(result[:, cols], faded[j % 2][:, cols], placed[j % 2][:, cols], ALU.add)
-                nc.sync.dma_start(out=out[P * j : P * (j + 1), cols], in_=result[:, cols])
+        def add_and_store(j, engine, rows):
+            for h in range(M_HALVES):
+                cols = slice(BANK * h, BANK * (h + 1))
+                engine.tensor_tensor(rows[:, cols], rows[:, cols], placed[j][:, cols], ALU.add)
+                nc.sync.dma_start(out=out[P * j : P * (j + 1), cols], in_=rows[:, cols])
 
         def middle(rows, words):
             return rows[:, M // 2 - words // 2 : M // 2 + words // 2]
@@ -254,17 +257,17 @@ def tile_attend_twopools_written_lean_kernel(
         gather_and_turn(1, staged[1][:], b_bank[1][:, :WORDS])
         gather_and_turn(2, staged[0][:], b_bank[1][:, WORDS:])
         read_and_place(0, a_bank[1])
-        fade_old(0)
+        fade_old(0, faded[0])
         group_and_quantize(1, 2, b_bank[1][:], middle(faded[1], 2 * WORDS))
-        fade_old(1)
-        add_and_store(0, 1)
-        gather_and_turn(3, staged[0][:], b_bank[0][:, :WORDS])
+        fade_old(1, faded[1])
+        add_and_store(0, nc.gpsimd, faded[0])
         read_and_place(1, a_bank[0])
-        fade_old(2)
-        group_and_quantize(3, 1, b_bank[0][:, :WORDS], middle(old_rows[2], WORDS))
-        add_and_store(1, 1)
+        add_and_store(1, nc.gpsimd, faded[1])
+        gather_and_turn(3, middle(old_rows[1], WORDS), b_bank[0][:, :WORDS])
+        group_and_quantize(3, 1, b_bank[0][:, :WORDS], first_staged[:])
         read_and_place(2, a_bank[1])
         read_and_place(3, a_bank[0])
-        fade_old(3)
-        add_and_store(2, 1)
-        add_and_store(3, 2)
+        fade_old(2, old_rows[1])
+        fade_old(3, old_rows[2])
+        add_and_store(2, nc.vector, old_rows[1])
+        add_and_store(3, nc.vector, old_rows[2])

@@ -24,7 +24,7 @@ E_TILES = E // P
 M_HALVES = M // BANK
 WORDS = I // 2
 HALF = I // 2
-LOAD_ORDER = (("v", 0), ("v", 1), ("v", 2), ("o", 0), ("o", 1), ("v", 3), ("o", 2), ("o", 3))
+LOAD_ORDER = (("v", 0), ("v", 1), ("v", 2), ("o", 0), ("v", 3), ("o", 1), ("o", 2), ("o", 3))
 
 
 def interleave(engine_copy, dst, src):
@@ -143,7 +143,7 @@ def tile_attend_twopools_written_lean_kernel(
         for h in range(M_HALVES):
             for j in range(PACK):
                 nc.tensor.transpose(
-                    fade_bank[h][:, P * j : P * (j + 1)], fade_cols[:, h, j : j + 1].to_broadcast([P, P]), ident[:]
+                    fade_bank[h][:, j:BANK:PACK], fade_cols[:, h, j : j + 1].to_broadcast([P, P]), ident[:]
                 )
 
         a_bank = [bank("a_bank%d" % n) for n in range(2)]
@@ -151,7 +151,9 @@ def tile_attend_twopools_written_lean_kernel(
         b_dealt = tile("b_dealt", [P, Q_TILES * I], F32)
         smaller = tile("smaller", [P, Q_TILES * I], F32)
         larger = tile("larger", [P, Q_TILES * I], F32)
-        faded = [tile("faded%d" % n, [P, M], F32) for n in range(2)]
+        first_faded = tile("first_faded", [P, M], F32)
+        second_work = tile("second_work", [P, M + WORDS], F32)
+        second_faded = [second_work[:, :BANK], second_work[:, BANK + WORDS :]]
 
         def scores(banks, n, which, codes, scales):
             slots = slice(HALF * n, HALF * (n + 1))
@@ -219,28 +221,25 @@ def tile_attend_twopools_written_lean_kernel(
             nc.scalar.copy(staged[j % 2][:], o_bank[:, :Q])
             nc.scalar.activation(placed[j][:].indirect(place_list[:]), staged[j % 2][:], COPY)
 
-        def fade_old(j, faded_rows):
-            for h in range(M_HALVES):
-                cols = slice(BANK * h, BANK * (h + 1))
-                nc.vector.tensor_tensor(
-                    faded_rows[:, cols].rearrange("e (p i) -> e p i", i=PACK),
-                    old_rows[j][:, cols].rearrange("e (p i) -> e p i", i=PACK),
-                    fade_bank[h][:].rearrange("e (i p) -> e p i", i=PACK),
-                    ALU.mult,
-                )
+        def halves(rows):
+            return [rows[:, BANK * h : BANK * (h + 1)] for h in range(M_HALVES)]
 
-        def add_and_store(j, engine, rows):
+        def fade_old(j, faded_halves):
             for h in range(M_HALVES):
-                cols = slice(BANK * h, BANK * (h + 1))
-                engine.tensor_tensor(rows[:, cols], rows[:, cols], placed[j][:, cols], ALU.add)
-                nc.sync.dma_start(out=out[P * j : P * (j + 1), cols], in_=rows[:, cols])
+                nc.vector.tensor_tensor(faded_halves[h], halves(old_rows[j])[h], fade_bank[h][:], ALU.mult)
+
+        def add_and_store(j, engine, faded_halves):
+            for h in range(M_HALVES):
+                engine.tensor_tensor(faded_halves[h], faded_halves[h], halves(placed[j])[h], ALU.add)
+                nc.sync.dma_start(out=out[P * j : P * (j + 1), BANK * h : BANK * (h + 1)], in_=faded_halves[h])
 
         def middle(rows, words):
-            return rows[:, M // 2 - words // 2 : M // 2 + words // 2]
+            width = rows.shape[1]
+            return rows[:, (width - words) // 2 : (width + words) // 2]
 
         gather_and_turn(0, first_staged[:], a_bank[0][:, :WORDS])
         group_and_quantize(0, 1, a_bank[0][:, :WORDS], middle(b_dealt, WORDS))
-        w_grouped = middle(faded[0], 2 * WORDS).bitcast(BF16)
+        w_grouped = middle(first_faded, 2 * WORDS).bitcast(BF16)
         for h in range(Q_TILES):
             nc.vector.scalar_tensor_tensor(
                 w_grouped[:, I * h : I * (h + 1)].rearrange("p (q t) -> p q t", t=PACK),
@@ -257,17 +256,17 @@ def tile_attend_twopools_written_lean_kernel(
         gather_and_turn(1, staged[1][:], b_bank[1][:, :WORDS])
         gather_and_turn(2, staged[0][:], b_bank[1][:, WORDS:])
         read_and_place(0, a_bank[1])
-        fade_old(0, faded[0])
-        group_and_quantize(1, 2, b_bank[1][:], middle(faded[1], 2 * WORDS))
-        fade_old(1, faded[1])
-        add_and_store(0, nc.gpsimd, faded[0])
+        fade_old(0, halves(first_faded))
+        group_and_quantize(1, 2, b_bank[1][:], middle(second_work, 2 * WORDS))
+        gather_and_turn(3, middle(second_work, WORDS), b_bank[0][:, :WORDS])
+        fade_old(1, second_faded)
+        add_and_store(0, nc.gpsimd, halves(first_faded))
         read_and_place(1, a_bank[0])
-        add_and_store(1, nc.gpsimd, faded[1])
-        gather_and_turn(3, middle(old_rows[1], WORDS), b_bank[0][:, :WORDS])
+        add_and_store(1, nc.gpsimd, second_faded)
         group_and_quantize(3, 1, b_bank[0][:, :WORDS], first_staged[:])
         read_and_place(2, a_bank[1])
         read_and_place(3, a_bank[0])
-        fade_old(2, old_rows[1])
-        fade_old(3, old_rows[2])
-        add_and_store(2, nc.vector, old_rows[1])
-        add_and_store(3, nc.vector, old_rows[2])
+        fade_old(2, halves(old_rows[1]))
+        fade_old(3, halves(old_rows[2]))
+        add_and_store(2, nc.vector, halves(old_rows[1]))
+        add_and_store(3, nc.vector, halves(old_rows[2]))

@@ -4,7 +4,7 @@ import concourse.mybir as mybir
 from concourse.masks import make_identity
 
 D, T, I, Q, E, U, M = 512, 2048, 512, 256, 512, 1024, 1024
-FLOPS = 2 * D * Q * I * 2 + 2 * I * E * Q
+FLOPS = 2 * (2 * D * Q * I) + 2 * I * E * Q
 
 F32 = mybir.dt.float32
 BF16 = mybir.dt.bfloat16
@@ -19,18 +19,23 @@ COPY = mybir.ActivationFunctionType.Copy
 P = 128
 PACK = 4
 BANK = 512
+QUADRANT = 32
+LIST_ROWS = 16
+RUN = 4
 Q_TILES = Q // P
 E_TILES = E // P
 M_HALVES = M // BANK
-WORDS = I // 2
-HALF = I // 2
-LOAD_ORDER = (("v", 0), ("v", 1), ("v", 2), ("o", 0), ("v", 3), ("o", 1), ("o", 2), ("o", 3))
+SLOT_HALVES = 2
+HALF = I // SLOT_HALVES
+PAIRS = I // 2
+SCALAR_NOTE_PLANES = 2
+SCALAR_VALUE_TILES = 3
 
 
-def interleave(engine_copy, dst, src):
+def interleave(engine_copy, grouped, planes):
     engine_copy(
-        dst.rearrange("p (c i) t -> p c t i", i=4),
-        src.rearrange("p t (c i) -> p c t i", i=4),
+        grouped.rearrange("p (c i) t -> p c t i", i=RUN),
+        planes.rearrange("p t (c i) -> p c t i", i=RUN),
     )
 
 
@@ -38,9 +43,9 @@ def quantize(nc, codes, scales, grouped):
     nc.vector.quantize_mx(out=codes.bitcast(FP8X4), scales=scales, in_=grouped)
 
 
-def product(nc, out, lhs_codes, lhs_scales, rhs_codes, rhs_scales):
+def product(nc, result, lhs_codes, lhs_scales, rhs_codes, rhs_scales):
     nc.tensor.matmul_mx(
-        out=out,
+        out=result,
         lhsT=lhs_codes.bitcast(FP8X4),
         lhsT_scale=lhs_scales,
         rhs=rhs_codes.bitcast(FP8X4),
@@ -48,6 +53,15 @@ def product(nc, out, lhs_codes, lhs_scales, rhs_codes, rhs_scales):
         start=True,
         stop=True,
     )
+
+
+def halves(rows):
+    return [rows[:, BANK * h : BANK * (h + 1)] for h in range(M_HALVES)]
+
+
+def middle(rows, width):
+    whole = rows.shape[1]
+    return rows[:, (whole - width) // 2 : (whole + width) // 2]
 
 
 def tile_attend_twopools_written_lean_kernel(
@@ -67,18 +81,18 @@ def tile_attend_twopools_written_lean_kernel(
         key_scale_pool = tile("key_scale_pool", [P, T], U8)
         nc.vector.memset(key_scale_pool[:].bitcast(I32), 0)
 
-        note_list = tile("note_list", [P, I // 16], U16)
+        note_list = tile("note_list", [P, I // LIST_ROWS], U16)
         nc.sync.dma_start(note_list[:], offs2)
-        token_list = tile("token_list", [P, I // 16], U16)
+        token_list = tile("token_list", [P, I // LIST_ROWS], U16)
         nc.sync.dma_start(token_list[:], offs)
         note_rows = notes.rearrange("(p t) u -> p t u", t=PACK)
         note_pool = [tile("note_pool%d" % t, [P, U], F32) for t in range(PACK)]
         for t in range(PACK):
             nc.sync.dma_start(out=note_pool[t][:], in_=note_rows[:, t, :])
-        for g in range(4):
+        for r in range(P // QUADRANT):
             nc.scalar.dma_start(
-                out=key_scale_pool[32 * g : 32 * g + 4, :].bitcast(I32),
-                in_=keys_scales[0, 4 * g : 4 * g + 4, :].bitcast(I32),
+                out=key_scale_pool[QUADRANT * r : QUADRANT * r + PACK, :].bitcast(I32),
+                in_=keys_scales[0, PACK * r : PACK * (r + 1), :].bitcast(I32),
             )
         q2_raw = tile("q2_raw", [P, PACK, Q], F32)
         nc.sync.dma_start(out=q2_raw[:], in_=query2.rearrange("(p t) q -> p t q", t=PACK))
@@ -88,24 +102,25 @@ def tile_attend_twopools_written_lean_kernel(
         nc.sync.dma_start(
             out=key_word_pool[:].bitcast(I32), in_=keys_words[0].rearrange("p n t -> p (n t)").bitcast(I32)
         )
-        place_list = tile("place_list", [P, Q // 16], U16)
+        place_list = tile("place_list", [P, Q // LIST_ROWS], U16)
         nc.sync.dma_start(place_list[:], offs3)
 
         factor_cols = tile("factor_cols", [P, PACK], F32)
-        nc.gpsimd.dma_start(out=factor_cols[:], in_=slot_factor.rearrange("o (p j) -> p (o j)", j=PACK))
+        nc.gpsimd.dma_start(out=factor_cols[:], in_=slot_factor.rearrange("o (p t) -> p (o t)", t=PACK))
         lam_cols = tile("lam_cols", [P, Q_TILES], F32)
         with nc.allow_non_contiguous_dma(reason="one float32 a partition and query tile"):
             nc.gpsimd.dma_start(out=lam_cols[:], in_=lam.rearrange("(h p) o -> p (h o)", p=P))
         fade_cols = tile("fade_cols", [P, M_HALVES, PACK], F32)
-        nc.gpsimd.dma_start(out=fade_cols[:], in_=fade.rearrange("o (h p j) -> p (o h) j", h=M_HALVES, j=PACK))
+        nc.gpsimd.dma_start(out=fade_cols[:], in_=fade.rearrange("o (h p t) -> p (o h) t", h=M_HALVES, t=PACK))
 
         val_pool = [tile("val_pool%d" % j, [P, T], F32) for j in range(E_TILES)]
         old_rows = [tile("old_rows%d" % j, [P, M], F32) for j in range(E_TILES)]
-        for kind, j in LOAD_ORDER:
-            if kind == "v":
-                nc.sync.dma_start(out=val_pool[j][:], in_=vals[P * j : P * (j + 1), :])
-            else:
-                nc.sync.dma_start(out=old_rows[j][:], in_=old[P * j : P * (j + 1), :])
+        val_loads = [(val_pool[j], vals, j) for j in range(E_TILES)]
+        old_loads = [(old_rows[j], old, j) for j in range(E_TILES)]
+        for rows, source, j in (
+            val_loads[:SCALAR_VALUE_TILES] + old_loads[:1] + val_loads[SCALAR_VALUE_TILES:] + old_loads[1:]
+        ):
+            nc.sync.dma_start(out=rows[:], in_=source[P * j : P * (j + 1), :])
 
         placed = [tile("placed%d" % j, [P, M], F32) for j in range(E_TILES)]
         for j in range(E_TILES):
@@ -119,71 +134,74 @@ def tile_attend_twopools_written_lean_kernel(
 
         note_planes = tile("note_planes", [P, PACK, I], BF16)
         for t in range(PACK):
-            picked = note_pool[t][:].indirect(note_list[:])
-            if t < 2:
-                nc.scalar.activation(note_planes[:, t, :], picked, COPY)
+            picked_notes = note_pool[t][:].indirect(note_list[:])
+            if t < SCALAR_NOTE_PLANES:
+                nc.scalar.activation(note_planes[:, t, :], picked_notes, COPY)
             else:
-                nc.vector.tensor_copy(note_planes[:, t, :], picked)
+                nc.vector.tensor_copy(note_planes[:, t, :], picked_notes)
         note_grouped = tile("note_grouped", [P, I, PACK], BF16)
         interleave(nc.vector.tensor_copy, note_grouped[:], note_planes[:])
         note_codes = tile("note_codes", [P, I], U32)
         note_scales = tile("note_scales", [P, I], U8)
         quantize(nc, note_codes[:], note_scales[:], note_grouped[:].rearrange("p s t -> p (s t)"))
 
-        q_codes, q_scales = [], []
-        for n, raw in enumerate((q2_raw, q1_raw)):
+        def quantize_queries(n, raw):
             grouped = tile("q_grouped%d" % n, [P, Q, PACK], BF16)
             interleave(nc.scalar.copy, grouped[:], raw[:])
-            q_codes.append(tile("q_codes%d" % n, [P, Q], U32))
-            q_scales.append(tile("q_scales%d" % n, [P, Q], U8))
-            quantize(nc, q_codes[n][:], q_scales[n][:], grouped[:].rearrange("p q t -> p (q t)"))
+            codes = tile("q_codes%d" % n, [P, Q], U32)
+            scales = tile("q_scales%d" % n, [P, Q], U8)
+            quantize(nc, codes[:], scales[:], grouped[:].rearrange("p q t -> p (q t)"))
+            return codes, scales
 
+        q2_codes, q2_scales = quantize_queries(0, q2_raw)
+        q1_codes, q1_scales = quantize_queries(1, q1_raw)
 
         fade_bank = [bank("fade_bank%d" % h) for h in range(M_HALVES)]
         for h in range(M_HALVES):
-            for j in range(PACK):
+            for t in range(PACK):
                 nc.tensor.transpose(
-                    fade_bank[h][:, j:BANK:PACK], fade_cols[:, h, j : j + 1].to_broadcast([P, P]), ident[:]
+                    fade_bank[h][:, t:BANK:PACK], fade_cols[:, h, t : t + 1].to_broadcast([P, P]), ident[:]
                 )
 
-        a_bank = [bank("a_bank%d" % n) for n in range(2)]
-        b_bank = [bank("b_bank%d" % n) for n in range(2)]
+        a_bank = [bank("a_bank%d" % n) for n in range(SLOT_HALVES)]
+        b_bank = [bank("b_bank%d" % n) for n in range(SLOT_HALVES)]
         b_dealt = tile("b_dealt", [P, Q_TILES * I], F32)
         smaller = tile("smaller", [P, Q_TILES * I], F32)
         larger = tile("larger", [P, Q_TILES * I], F32)
         first_faded = tile("first_faded", [P, M], F32)
-        second_work = tile("second_work", [P, M + WORDS], F32)
-        second_faded = [second_work[:, :BANK], second_work[:, BANK + WORDS :]]
+        second_work = tile("second_work", [P, M + PAIRS], F32)
+        second_faded = [second_work[:, :BANK], second_work[:, BANK + PAIRS :]]
 
-        def scores(banks, n, which, codes, scales):
+        def score_half(banks, n, row_codes, row_scales, slot_codes, slot_scales):
             slots = slice(HALF * n, HALF * (n + 1))
             for h in range(Q_TILES):
-                rows = slice(P * h, P * (h + 1))
+                q_rows = slice(P * h, P * (h + 1))
                 product(
                     nc,
                     banks[n][:, HALF * h : HALF * (h + 1)],
-                    q_codes[which][:, rows],
-                    q_scales[which][:, rows],
-                    codes[:, slots],
-                    scales[:, slots],
+                    row_codes[:, q_rows],
+                    row_scales[:, q_rows],
+                    slot_codes[:, slots],
+                    slot_scales[:, slots],
                 )
 
-        def dealt_from_bank(bank_tile):
-            return bank_tile[:].rearrange("q (h p t) -> q h t p", h=Q_TILES, t=PACK)
+        def dealt_from_bank(score_bank):
+            return score_bank[:].rearrange("q (h p t) -> q h t p", h=Q_TILES, t=PACK)
 
-        def dealt_half(rows, n):
-            return rows[:].rearrange("q (h t p) -> q h t p", h=Q_TILES, t=PACK)[:, :, :, P // 2 * n : P // 2 * (n + 1)]
+        def dealt_half(dealt, n):
+            width = P // SLOT_HALVES
+            return dealt[:].rearrange("q (h t p) -> q h t p", h=Q_TILES, t=PACK)[:, :, :, width * n : width * (n + 1)]
 
-        for n in range(2):
-            scores(b_bank, n, 0, note_codes, note_scales)
+        for n in range(SLOT_HALVES):
+            score_half(b_bank, n, q2_codes, q2_scales, note_codes, note_scales)
             nc.scalar.copy(dealt_half(b_dealt, n), dealt_from_bank(b_bank[n]))
-        for n in range(2):
-            entries = token_list[:, HALF // 16 * n : HALF // 16 * (n + 1)]
+        for n in range(SLOT_HALVES):
+            entries = token_list[:, HALF // LIST_ROWS * n : HALF // LIST_ROWS * (n + 1)]
             nc.vector.tensor_copy(key_codes[:, HALF * n : HALF * (n + 1)], key_word_pool[:].indirect(entries))
-            scores(a_bank, n, 1, key_codes, key_scales)
-        for n in range(2):
-            for dst, op in ((smaller, ALU.min), (larger, ALU.max)):
-                nc.vector.tensor_tensor(dealt_half(dst, n), dealt_from_bank(a_bank[n]), dealt_half(b_dealt, n), op)
+            score_half(a_bank, n, q1_codes, q1_scales, key_codes, key_scales)
+        for n in range(SLOT_HALVES):
+            for dealt, op in ((smaller, ALU.min), (larger, ALU.max)):
+                nc.vector.tensor_tensor(dealt_half(dealt, n), dealt_from_bank(a_bank[n]), dealt_half(b_dealt, n), op)
         for h in range(Q_TILES):
             cols = slice(I * h, I * (h + 1))
             nc.vector.scalar_tensor_tensor(
@@ -193,19 +211,20 @@ def tile_attend_twopools_written_lean_kernel(
                 nc.tensor.transpose(
                     b_bank[h][:, P * t : P * (t + 1)], larger[:, I * h + P * t : I * h + P * (t + 1)], ident[:]
                 )
+
         v_codes = tile("v_codes", [P, E], U32)
         v_scales = tile("v_scales", [P, E], U8)
-        staged = [tile("staged%d" % n, [P, WORDS], F32) for n in range(2)]
-        first_staged = tile("first_staged", [P, WORDS], F32)
+        staged = [tile("staged%d" % n, [P, PAIRS], F32) for n in range(2)]
+        first_staged = tile("first_staged", [P, PAIRS], F32)
 
-        def gather_and_turn(j, words, turned):
-            picked = val_pool[j][:].indirect(token_list[:])
-            if j < E_TILES - 1:
-                nc.scalar.activation(words.bitcast(BF16), picked, COPY)
+        def gather_and_turn(j, pairs, turned):
+            picked_vals = val_pool[j][:].indirect(token_list[:])
+            if j < SCALAR_VALUE_TILES:
+                nc.scalar.activation(pairs.bitcast(BF16), picked_vals, COPY)
             else:
-                nc.vector.tensor_copy(words.bitcast(BF16), picked)
+                nc.vector.tensor_copy(pairs.bitcast(BF16), picked_vals)
             for u in range(2):
-                nc.tensor.transpose(turned[:, P * u : P * (u + 1)], words[:, u:WORDS:2], ident[:])
+                nc.tensor.transpose(turned[:, P * u : P * (u + 1)], pairs[:, u:PAIRS:2], ident[:])
 
         def group_and_quantize(first, count, turned, grouped):
             nc.vector.tensor_copy(
@@ -221,28 +240,22 @@ def tile_attend_twopools_written_lean_kernel(
             nc.scalar.copy(staged[j % 2][:], o_bank[:, :Q])
             nc.scalar.activation(placed[j][:].indirect(place_list[:]), staged[j % 2][:], COPY)
 
-        def halves(rows):
-            return [rows[:, BANK * h : BANK * (h + 1)] for h in range(M_HALVES)]
-
         def fade_old(j, faded_halves):
             for h in range(M_HALVES):
                 nc.vector.tensor_tensor(faded_halves[h], halves(old_rows[j])[h], fade_bank[h][:], ALU.mult)
 
-        def add_and_store(j, engine, faded_halves):
+        def add_and_store(j, engine, faded_halves, result_halves):
             for h in range(M_HALVES):
-                engine.tensor_tensor(faded_halves[h], faded_halves[h], halves(placed[j])[h], ALU.add)
-                nc.sync.dma_start(out=out[P * j : P * (j + 1), BANK * h : BANK * (h + 1)], in_=faded_halves[h])
+                engine.tensor_tensor(result_halves[h], faded_halves[h], halves(placed[j])[h], ALU.add)
+                nc.sync.dma_start(out=out[P * j : P * (j + 1), BANK * h : BANK * (h + 1)], in_=result_halves[h])
 
-        def middle(rows, words):
-            width = rows.shape[1]
-            return rows[:, (width - words) // 2 : (width + words) // 2]
+        gather_and_turn(0, first_staged[:], a_bank[0][:, :PAIRS])
+        group_and_quantize(0, 1, a_bank[0][:, :PAIRS], middle(b_dealt, PAIRS))
 
-        gather_and_turn(0, first_staged[:], a_bank[0][:, :WORDS])
-        group_and_quantize(0, 1, a_bank[0][:, :WORDS], middle(b_dealt, WORDS))
-        w_grouped = middle(first_faded, 2 * WORDS).bitcast(BF16)
+        w_grouped = middle(first_faded, Q * PACK // 2).bitcast(BF16)
         for h in range(Q_TILES):
             nc.vector.scalar_tensor_tensor(
-                w_grouped[:, I * h : I * (h + 1)].rearrange("p (q t) -> p q t", t=PACK),
+                w_grouped[:, P * PACK * h : P * PACK * (h + 1)].rearrange("p (q t) -> p q t", t=PACK),
                 b_bank[h][:].rearrange("p (t q) -> p q t", t=PACK),
                 0.0,
                 factor_cols[:].unsqueeze(1).to_broadcast([P, P, PACK]),
@@ -253,20 +266,20 @@ def tile_attend_twopools_written_lean_kernel(
         w_scales = tile("w_scales", [P, Q], U8)
         quantize(nc, w_codes[:], w_scales[:], w_grouped)
 
-        gather_and_turn(1, staged[1][:], b_bank[1][:, :WORDS])
-        gather_and_turn(2, staged[0][:], b_bank[1][:, WORDS:])
+        gather_and_turn(1, staged[1][:], b_bank[1][:, :PAIRS])
+        gather_and_turn(2, staged[0][:], b_bank[1][:, PAIRS:])
         read_and_place(0, a_bank[1])
         fade_old(0, halves(first_faded))
-        group_and_quantize(1, 2, b_bank[1][:], middle(second_work, 2 * WORDS))
-        gather_and_turn(3, middle(second_work, WORDS), b_bank[0][:, :WORDS])
+        group_and_quantize(1, 2, b_bank[1][:], middle(second_work, 2 * PAIRS))
+        gather_and_turn(3, middle(second_work, PAIRS), b_bank[0][:, :PAIRS])
         fade_old(1, second_faded)
-        add_and_store(0, nc.gpsimd, halves(first_faded))
+        add_and_store(0, nc.gpsimd, halves(first_faded), halves(first_faded))
         read_and_place(1, a_bank[0])
-        add_and_store(1, nc.gpsimd, second_faded)
-        group_and_quantize(3, 1, b_bank[0][:, :WORDS], first_staged[:])
+        group_and_quantize(3, 1, b_bank[0][:, :PAIRS], middle(smaller, PAIRS))
+        add_and_store(1, nc.gpsimd, second_faded, halves(smaller))
         read_and_place(2, a_bank[1])
         read_and_place(3, a_bank[0])
         fade_old(2, halves(old_rows[1]))
         fade_old(3, halves(old_rows[2]))
-        add_and_store(2, nc.vector, halves(old_rows[1]))
-        add_and_store(3, nc.vector, halves(old_rows[2]))
+        add_and_store(2, nc.vector, halves(old_rows[1]), halves(old_rows[1]))
+        add_and_store(3, nc.vector, halves(old_rows[2]), halves(old_rows[2]))

from contextlib import ExitStack

import concourse.mybir as mybir
from concourse.masks import make_identity

D, T, I, Q, E, U, M = 512, 2048, 512, 256, 512, 1024, 1024
FLOPS = 2 * (2 * D * Q * I) + 2 * I * E * Q

F32 = mybir.dt.float32
BF16 = mybir.dt.bfloat16
I32 = mybir.dt.int32
U32 = mybir.dt.uint32
U16 = mybir.dt.uint16
U8 = mybir.dt.uint8
FP8X4 = mybir.dt.float8_e4m3fn_x4
ALU = mybir.AluOpType
COPY = mybir.ActivationFunctionType.Copy

P = 128
PACK = 4
BANK = 512
QUADRANT = 32
LIST_ROWS = 16
RUN = 4
Q_TILES = Q // P
E_TILES = E // P
M_HALVES = M // BANK
SLOT_HALVES = 2
HALF = I // SLOT_HALVES
PAIRS = I // 2
SCALAR_NOTE_PLANES = 2
SCALAR_VALUE_TILES = 3


def interleave(engine_copy, grouped, planes):
    engine_copy(
        grouped.rearrange("p (c i) t -> p c t i", i=RUN),
        planes.rearrange("p t (c i) -> p c t i", i=RUN),
    )


def quantize(nc, codes, scales, grouped):
    nc.vector.quantize_mx(out=codes.bitcast(FP8X4), scales=scales, in_=grouped)


def product(nc, result, lhs_codes, lhs_scales, rhs_codes, rhs_scales):
    nc.tensor.matmul_mx(
        out=result,
        lhsT=lhs_codes.bitcast(FP8X4),
        lhsT_scale=lhs_scales,
        rhs=rhs_codes.bitcast(FP8X4),
        rhs_scale=rhs_scales,
        start=True,
        stop=True,
    )


def halves(rows):
    return [rows[:, BANK * h : BANK * (h + 1)] for h in range(M_HALVES)]


def middle(rows, width):
    whole = rows.shape[1]
    return rows[:, (whole - width) // 2 : (whole + width) // 2]


def tile_attend_twopools_written_lean_kernel(
    tc, query, keys_words, keys_scales, query2, notes, lam, slot_factor, vals, old, fade, offs, offs2, offs3, out
):
    nc = tc.nc
    with ExitStack() as ctx:
        sb = ctx.enter_context(tc.tile_pool(name="sb", bufs=1))
        ps = ctx.enter_context(tc.psum_pool(name="ps", bufs=1))

        def tile(name, shape, dtype):
            return sb.tile(shape, dtype, name=name, align_bytes=64)

        def bank(name):
            return ps.tile([P, BANK], F32, name=name)

        key_scale_pool = tile("key_scale_pool", [P, T], U8)
        nc.vector.memset(key_scale_pool[:].bitcast(I32), 0)

        note_list = tile("note_list", [P, I // LIST_ROWS], U16)
        nc.sync.dma_start(note_list[:], offs2)
        token_list = tile("token_list", [P, I // LIST_ROWS], U16)
        nc.sync.dma_start(token_list[:], offs)
        note_rows = notes.rearrange("(p t) u -> p t u", t=PACK)
        note_pool = [tile("note_pool%d" % t, [P, U], F32) for t in range(PACK)]
        for t in range(PACK):
            nc.sync.dma_start(out=note_pool[t][:], in_=note_rows[:, t, :])
        for r in range(P // QUADRANT):
            nc.scalar.dma_start(
                out=key_scale_pool[QUADRANT * r : QUADRANT * r + PACK, :].bitcast(I32),
                in_=keys_scales[0, PACK * r : PACK * (r + 1), :].bitcast(I32),
            )
        q2_raw = tile("q2_raw", [P, PACK, Q], F32)
        nc.sync.dma_start(out=q2_raw[:], in_=query2.rearrange("(p t) q -> p t q", t=PACK))
        q1_raw = tile("q1_raw", [P, PACK, Q], F32)
        nc.sync.dma_start(out=q1_raw[:], in_=query.rearrange("(p t) q -> p t q", t=PACK))
        key_word_pool = tile("key_word_pool", [P, T], U32)
        nc.sync.dma_start(
            out=key_word_pool[:].bitcast(I32), in_=keys_words[0].rearrange("p n t -> p (n t)").bitcast(I32)
        )
        place_list = tile("place_list", [P, Q // LIST_ROWS], U16)
        nc.sync.dma_start(place_list[:], offs3)

        factor_cols = tile("factor_cols", [P, PACK], F32)
        nc.gpsimd.dma_start(out=factor_cols[:], in_=slot_factor.rearrange("o (p t) -> p (o t)", t=PACK))
        lam_cols = tile("lam_cols", [P, Q_TILES], F32)
        with nc.allow_non_contiguous_dma(reason="one float32 a partition and query tile"):
            nc.gpsimd.dma_start(out=lam_cols[:], in_=lam.rearrange("(h p) o -> p (h o)", p=P))
        fade_cols = tile("fade_cols", [P, M_HALVES, PACK], F32)
        nc.gpsimd.dma_start(out=fade_cols[:], in_=fade.rearrange("o (h p t) -> p (o h) t", h=M_HALVES, t=PACK))

        val_pool = [tile("val_pool%d" % j, [P, T], F32) for j in range(E_TILES)]
        old_rows = [tile("old_rows%d" % j, [P, M], F32) for j in range(E_TILES)]
        val_loads = [(val_pool[j], vals, j) for j in range(E_TILES)]
        old_loads = [(old_rows[j], old, j) for j in range(E_TILES)]
        for rows, source, j in (
            val_loads[:SCALAR_VALUE_TILES] + old_loads[:1] + val_loads[SCALAR_VALUE_TILES:] + old_loads[1:]
        ):
            nc.sync.dma_start(out=rows[:], in_=source[P * j : P * (j + 1), :])

        placed = [tile("placed%d" % j, [P, M], F32) for j in range(E_TILES)]
        for j in range(E_TILES):
            nc.vector.memset(placed[j][:], 0.0)
        ident = tile("ident", [P, P], F32)
        make_identity(nc, ident[:])

        key_codes = tile("key_codes", [P, I], U32)
        key_scales = tile("key_scales", [P, I], U8)
        nc.vector.tensor_copy(key_scales[:], key_scale_pool[:].indirect(token_list[:]))

        note_planes = tile("note_planes", [P, PACK, I], BF16)
        for t in range(PACK):
            picked_notes = note_pool[t][:].indirect(note_list[:])
            if t < SCALAR_NOTE_PLANES:
                nc.scalar.activation(note_planes[:, t, :], picked_notes, COPY)
            else:
                nc.vector.tensor_copy(note_planes[:, t, :], picked_notes)
        note_grouped = tile("note_grouped", [P, I, PACK], BF16)
        interleave(nc.vector.tensor_copy, note_grouped[:], note_planes[:])
        note_codes = tile("note_codes", [P, I], U32)
        note_scales = tile("note_scales", [P, I], U8)
        quantize(nc, note_codes[:], note_scales[:], note_grouped[:].rearrange("p s t -> p (s t)"))

        def quantize_queries(n, raw):
            grouped = tile("q_grouped%d" % n, [P, Q, PACK], BF16)
            interleave(nc.scalar.copy, grouped[:], raw[:])
            codes = tile("q_codes%d" % n, [P, Q], U32)
            scales = tile("q_scales%d" % n, [P, Q], U8)
            quantize(nc, codes[:], scales[:], grouped[:].rearrange("p q t -> p (q t)"))
            return codes, scales

        q2_codes, q2_scales = quantize_queries(0, q2_raw)
        q1_codes, q1_scales = quantize_queries(1, q1_raw)

        fade_bank = [bank("fade_bank%d" % h) for h in range(M_HALVES)]
        for h in range(M_HALVES):
            for t in range(PACK):
                nc.tensor.transpose(
                    fade_bank[h][:, t:BANK:PACK], fade_cols[:, h, t : t + 1].to_broadcast([P, P]), ident[:]
                )

        a_bank = [bank("a_bank%d" % n) for n in range(SLOT_HALVES)]
        b_bank = [bank("b_bank%d" % n) for n in range(SLOT_HALVES)]
        b_dealt = tile("b_dealt", [P, Q_TILES * I], F32)
        smaller = tile("smaller", [P, Q_TILES * I], F32)
        larger = tile("larger", [P, Q_TILES * I], F32)
        first_faded = tile("first_faded", [P, M], F32)
        second_work = tile("second_work", [P, M + PAIRS], F32)
        second_faded = [second_work[:, :BANK], second_work[:, BANK + PAIRS :]]

        def score_half(banks, n, row_codes, row_scales, slot_codes, slot_scales):
            slots = slice(HALF * n, HALF * (n + 1))
            for h in range(Q_TILES):
                q_rows = slice(P * h, P * (h + 1))
                product(
                    nc,
                    banks[n][:, HALF * h : HALF * (h + 1)],
                    row_codes[:, q_rows],
                    row_scales[:, q_rows],
                    slot_codes[:, slots],
                    slot_scales[:, slots],
                )

        def dealt_from_bank(score_bank):
            return score_bank[:].rearrange("q (h p t) -> q h t p", h=Q_TILES, t=PACK)

        def dealt_half(dealt, n):
            width = P // SLOT_HALVES
            return dealt[:].rearrange("q (h t p) -> q h t p", h=Q_TILES, t=PACK)[:, :, :, width * n : width * (n + 1)]

        for n in range(SLOT_HALVES):
            score_half(b_bank, n, q2_codes, q2_scales, note_codes, note_scales)
            nc.scalar.copy(dealt_half(b_dealt, n), dealt_from_bank(b_bank[n]))
        for n in range(SLOT_HALVES):
            entries = token_list[:, HALF // LIST_ROWS * n : HALF // LIST_ROWS * (n + 1)]
            nc.vector.tensor_copy(key_codes[:, HALF * n : HALF * (n + 1)], key_word_pool[:].indirect(entries))
            score_half(a_bank, n, q1_codes, q1_scales, key_codes, key_scales)
        for n in range(SLOT_HALVES):
            for dealt, op in ((smaller, ALU.min), (larger, ALU.max)):
                nc.vector.tensor_tensor(dealt_half(dealt, n), dealt_from_bank(a_bank[n]), dealt_half(b_dealt, n), op)
        for h in range(Q_TILES):
            cols = slice(I * h, I * (h + 1))
            nc.vector.scalar_tensor_tensor(
                larger[:, cols], smaller[:, cols], lam_cols[:, h : h + 1], larger[:, cols], ALU.mult, ALU.add
            )
            for t in range(PACK):
                nc.tensor.transpose(
                    b_bank[h][:, P * t : P * (t + 1)], larger[:, I * h + P * t : I * h + P * (t + 1)], ident[:]
                )

        v_codes = tile("v_codes", [P, E], U32)
        v_scales = tile("v_scales", [P, E], U8)
        staged = [tile("staged%d" % n, [P, PAIRS], F32) for n in range(2)]
        first_staged = tile("first_staged", [P, PAIRS], F32)

        def gather_and_turn(j, pairs, turned):
            picked_vals = val_pool[j][:].indirect(token_list[:])
            if j < SCALAR_VALUE_TILES:
                nc.scalar.activation(pairs.bitcast(BF16), picked_vals, COPY)
            else:
                nc.vector.tensor_copy(pairs.bitcast(BF16), picked_vals)
            for u in range(2):
                nc.tensor.transpose(turned[:, P * u : P * (u + 1)], pairs[:, u:PAIRS:2], ident[:])

        def group_and_quantize(first, count, turned, grouped):
            nc.vector.tensor_copy(
                grouped.rearrange("p (j e u) -> p j e u", j=count, u=2),
                turned.rearrange("p (j u e) -> p j e u", j=count, u=2),
            )
            cols = slice(P * first, P * (first + count))
            quantize(nc, v_codes[:, cols], v_scales[:, cols], grouped.bitcast(BF16))

        def read_and_place(j, o_bank):
            cols = slice(P * j, P * (j + 1))
            product(nc, o_bank[:, :Q], v_codes[:, cols], v_scales[:, cols], w_codes[:], w_scales[:])
            nc.scalar.copy(staged[j % 2][:], o_bank[:, :Q])
            nc.scalar.activation(placed[j][:].indirect(place_list[:]), staged[j % 2][:], COPY)

        def fade_old(j, faded_halves):
            for h in range(M_HALVES):
                nc.vector.tensor_tensor(faded_halves[h], halves(old_rows[j])[h], fade_bank[h][:], ALU.mult)

        def add_and_store(j, engine, faded_halves, result_halves):
            for h in range(M_HALVES):
                engine.tensor_tensor(result_halves[h], faded_halves[h], halves(placed[j])[h], ALU.add)
                nc.sync.dma_start(out=out[P * j : P * (j + 1), BANK * h : BANK * (h + 1)], in_=result_halves[h])

        gather_and_turn(0, first_staged[:], a_bank[0][:, :PAIRS])
        group_and_quantize(0, 1, a_bank[0][:, :PAIRS], middle(b_dealt, PAIRS))

        w_grouped = middle(first_faded, Q * PACK // 2).bitcast(BF16)
        for h in range(Q_TILES):
            nc.vector.scalar_tensor_tensor(
                w_grouped[:, P * PACK * h : P * PACK * (h + 1)].rearrange("p (q t) -> p q t", t=PACK),
                b_bank[h][:].rearrange("p (t q) -> p q t", t=PACK),
                0.0,
                factor_cols[:].unsqueeze(1).to_broadcast([P, P, PACK]),
                ALU.max,
                ALU.mult,
            )
        w_codes = tile("w_codes", [P, Q], U32)
        w_scales = tile("w_scales", [P, Q], U8)
        quantize(nc, w_codes[:], w_scales[:], w_grouped)

        gather_and_turn(1, staged[1][:], b_bank[1][:, :PAIRS])
        gather_and_turn(2, staged[0][:], b_bank[1][:, PAIRS:])
        read_and_place(0, a_bank[1])
        fade_old(0, halves(first_faded))
        group_and_quantize(1, 2, b_bank[1][:], middle(second_work, 2 * PAIRS))
        gather_and_turn(3, middle(second_work, PAIRS), b_bank[0][:, :PAIRS])
        fade_old(1, second_faded)
        add_and_store(0, nc.gpsimd, halves(first_faded), halves(first_faded))
        read_and_place(1, a_bank[0])
        group_and_quantize(3, 1, b_bank[0][:, :PAIRS], middle(smaller, PAIRS))
        add_and_store(1, nc.gpsimd, second_faded, halves(smaller))
        read_and_place(2, a_bank[1])
        read_and_place(3, a_bank[0])
        fade_old(2, halves(old_rows[1]))
        fade_old(3, halves(old_rows[2]))
        add_and_store(2, nc.vector, halves(old_rows[1]), halves(old_rows[1]))
        add_and_store(3, nc.vector, halves(old_rows[2]), halves(old_rows[2]))
